import numpy as np
import ml_dtypes


def mxq(x, axis, fmt="e4m3"):
    dtype, down = {"e4m3": (ml_dtypes.float8_e4m3fn, 7), "e5m2": (ml_dtypes.float8_e5m2, 14)}[fmt]
    v = np.moveaxis(np.asarray(x, np.float32).astype(ml_dtypes.bfloat16).astype(np.float64), axis, -1)
    blocks = v.reshape(v.shape[:-1] + (-1, 32))
    amax = np.abs(blocks).max(-1, keepdims=True)
    byte = np.maximum(np.where(amax > 0, np.frexp(amax)[1] - 1 + 127, 0) - down, 1)
    scale = np.exp2(byte - 127.0)
    codes = (blocks / scale).astype(np.float32).astype(dtype).astype(np.float64)
    return np.moveaxis((codes * scale).reshape(v.shape), -1, axis)


WIDE = False


def mx_kscale(k):
    if not WIDE:
        return np.ones(k)
    levels = np.array([10, -10, 5, -5, 0])
    if k % 512:
        return np.exp2(np.random.permutation(np.resize(levels, k // 32))).repeat(32)
    a = np.empty((k // 512, 16))
    for p in range(k // 512):
        a[p, :8] = np.random.permutation(np.resize(levels, 8))
        for g in range(8):
            far = levels[np.abs(levels - a[p, g]) >= 10]
            a[p, g + 8] = far[np.random.randint(len(far))]
    return np.exp2(a.ravel()).repeat(32)


def f64(x):
    return np.asarray(x).astype(np.float64)


def striped(idx):
    return np.tile(idx.reshape(-1, 16).T, (8, 1)).astype(np.uint16)


def unstriped(offs):
    return offs[:16].T.reshape(-1).astype(np.int64)


def pack_weight(w):
    k, n = w.shape
    w = f64(np.asarray(w, np.float32).astype(ml_dtypes.bfloat16)).reshape(k // 32, 32, n)
    amax = np.abs(w).max(1)
    byte = np.clip(np.where(amax > 0, np.frexp(amax)[1] - 1 + 127 - 7, 1), 1, 254)
    scaled = (w * np.exp2(127.0 - byte)[:, None, :]).reshape(k, n).astype(np.float32)
    words = np.ascontiguousarray(scaled.reshape(k // 512, 128, 4, n).transpose(0, 1, 3, 2)).astype(ml_dtypes.float8_e4m3fn).view(np.uint8)
    return words, np.ascontiguousarray(byte.astype(np.uint8).reshape(k // 512, 16, n))


def unpack_weight(words, scales):
    g, p, n, _ = words.shape
    vals = np.ascontiguousarray(words).view(ml_dtypes.float8_e4m3fn).astype(np.float64) * np.repeat(np.exp2(scales.astype(np.float64) - 127.0), 8, axis=1)[..., None]
    return vals.transpose(0, 1, 3, 2).reshape(g * 512, n)


def planes(y):
    n, m = y.shape
    v = y.astype(np.float32).astype(ml_dtypes.bfloat16).astype(np.float64).reshape(n // 32, 32, m)
    top = np.abs(v).max(1)
    byte = np.clip(np.where(top > 0, np.frexp(top)[1] - 1 + 127 - 7, 1), 1, 254)
    codes = (v * np.exp2(127.0 - byte)[:, None, :]).reshape(n, m).astype(np.float32).astype(ml_dtypes.float8_e4m3fn).view(np.uint8)
    words = codes.reshape(n // 512, 128, 4, m).transpose(0, 1, 3, 2)
    return np.ascontiguousarray(words), np.ascontiguousarray(byte.astype(np.uint8).reshape(n // 512, 16, m))


def sigmoid(v):
    return 1.0 / (1.0 + np.exp(-np.maximum(v, -700.0)))


K, T, S, N, H, W, G = 512, 1024, 512, 512, 512, 2048, 1024


def setup_inputs():
    n = np.random.standard_normal
    s = mx_kscale(K)[:, None]
    u = mx_kscale(H)
    packed_xT = pack_weight(n((K, T)) * s)
    packed_eT = pack_weight(n((K, W)) * s)
    packed_dT = pack_weight(n((K, G)) * s)
    return {
        "x_words": packed_xT[0],
        "x_scales": packed_xT[1],
        "w1": (n((K, N)) / np.sqrt(K) / s).astype(np.float32),
        "e_words": packed_eT[0],
        "e_scales": packed_eT[1],
        "w2": (n((K, N)) / np.sqrt(K) / s).astype(np.float32),
        "d_words": packed_dT[0],
        "d_scales": packed_dT[1],
        "w3": (n((K, N)) / np.sqrt(K) / s).astype(np.float32),
        "unit": (np.random.uniform(0.6, 1.4, (H, 1)) * u[:, None]).astype(np.float32),
        "w4": (n((H, N)) / np.sqrt(H) / u[:, None]).astype(np.float32),
        "offs": striped(np.random.permutation(T)[:S]),
        "ovl": striped(np.random.permutation(W)[:S]),
        "lab": striped(np.random.permutation(G)[:S]),
        "sh1": striped(np.random.permutation(S)),
        "px": striped(np.random.permutation(S)),
    }


def reference(x_words, x_scales, w1, e_words, e_scales, w2, d_words, d_scales, w3, unit, w4, offs, ovl, lab, sh1, px):
    d_lab = unpack_weight(d_words, d_scales)[:, unstriped(lab)]
    yd = mxq(f64(w3), 0, "e4m3").T @ d_lab
    alp = sigmoid(2.0 * yd)
    xq = unpack_weight(x_words, x_scales)[:, unstriped(offs)]
    y = mxq(f64(w1), 0, "e4m3").T @ xq
    e_ovl = unpack_weight(e_words, e_scales)[:, unstriped(ovl)]
    ye = mxq(f64(w2), 0, "e4m3").T @ e_ovl
    es1 = ye[:, unstriped(sh1)]
    cmp1 = np.maximum(y, 0.8 * es1)
    cov = alp * yd + (-1.0 * alp + 1.0) * cmp1
    zp = cov[:, unstriped(px)]
    hid = f64(unit) * (zp * alp)
    out_0 = mxq(f64(w4), 0, "e4m3").T @ mxq(hid, 0, "e4m3")
    return (out_0,) + planes(out_0)

@@ -1,0 +1,235 @@
+from contextlib import ExitStack
+
+import concourse.mybir as mybir
+
+F32 = mybir.dt.float32
+BF16 = mybir.dt.bfloat16
+I32 = mybir.dt.int32
+U32 = mybir.dt.uint32
+U16 = mybir.dt.uint16
+U8 = mybir.dt.uint8
+FP8X4 = mybir.dt.float8_e4m3fn_x4
+ALU = mybir.AluOpType
+ACT = mybir.ActivationFunctionType
+
+P = 128
+PACK = 4
+K = 512
+S = 512
+HALF = 256
+CHUNKS = 4
+CH = S // CHUNKS
+
+FLOPS = 4 * 2 * K * K * S
+
+
+def tile_picked_ymapovl_alpha_po_kernel(
+    tc, x_words, x_scales, w1, e_words, e_scales, w2, d_words, d_scales, w3, unit, w4,
+    offs, ovl, lab, sh1, px, out_0, out_1, out_2,
+):
+    nc = tc.nc
+    with ExitStack() as ctx:
+        keep = ctx.enter_context(tc.tile_pool(name="keep", bufs=1))
+        psum = ctx.enter_context(tc.psum_pool(name="psum", bufs=1))
+
+        def sb(name, shape, dtype):
+            return keep.tile(shape, dtype, name=name, align_bytes=64)
+
+        def load_list(name, src):
+            t = keep.tile([P, S // 16], U16, name=name)
+            nc.sync.dma_start(t[:], src)
+            return t
+
+        def scale_window(name, cols, engine):
+            t = sb(name, [P, cols], U8)
+            engine.memset(t[:].bitcast(I32), 0)
+            return t
+
+        def load_scales_spread(t, src, cols):
+            for q in range(4):
+                rows = src[0, 4 * q : 4 * q + 4, :].bitcast(I32)
+                nc.sync.dma_start(t[32 * q : 32 * q + 32, :].bitcast(I32), rows.unsqueeze(0).broadcast_to([8, 4, cols // 4]))
+
+        def load_scales(t, src, queue):
+            for q in range(4):
+                queue.dma_start(t[32 * q : 32 * q + 4, :].bitcast(I32), src[0, 4 * q : 4 * q + 4, :].bitcast(I32))
+
+        def load_words(name, src, cols):
+            t = sb(name, [P, cols], U32)
+            nc.sync.dma_start(t[:].bitcast(I32), src[0].rearrange("p n t -> p (n t)").bitcast(I32))
+            return t
+
+        def load_weight_half(name, w, h):
+            t = sb(name + "_raw%d" % h, [P, PACK, HALF], F32)
+            nc.sync.dma_start(t[:], w.rearrange("(p j) c -> p j c", j=PACK)[:, :, h * HALF : (h + 1) * HALF])
+            return t
+
+        def round_weight_half(engine, grouped, raw, h):
+            m = HALF // PACK
+            dst = grouped[:].rearrange("p (t m j) -> p m t j", t=PACK, j=PACK)[:, h * m : (h + 1) * m]
+            src = raw[:].rearrange("p j (m t) -> p m t j", t=PACK)
+            if engine == "scalar":
+                nc.scalar.copy(dst, src)
+            elif engine == "gpsimd":
+                nc.gpsimd.tensor_scalar(dst, src, 1.0, 0.0, ALU.mult, ALU.add)
+            else:
+                nc.vector.tensor_copy(dst, src)
+
+        def fetch(engine, dst, window, offsets):
+            if engine == "scalar":
+                nc.scalar.activation(dst, window[:].indirect(offsets), ACT.Copy)
+            else:
+                nc.vector.tensor_copy(dst, window[:].indirect(offsets))
+
+        def quantize(name, grouped, cols):
+            codes = sb(name + "_codes", [P, cols], U32)
+            scales = sb(name + "_scales", [P, cols], U8)
+            nc.vector.quantize_mx(out=codes[:].bitcast(FP8X4), scales=scales[:], in_=grouped)
+            return codes, scales
+
+        def gather(name, window, offsets, dtype):
+            t = sb(name, [P, S], dtype)
+            nc.vector.tensor_copy(t[:], window[:].indirect(offsets[:]))
+            return t
+
+        def product(dst, w, t, rhs_codes, rhs_scales):
+            cols = slice(t * P, (t + 1) * P)
+            nc.tensor.matmul_mx(
+                out=dst, lhsT=w[0][:, cols].bitcast(FP8X4), lhsT_scale=w[1][:, cols],
+                rhs=rhs_codes.bitcast(FP8X4), rhs_scale=rhs_scales, start=True, stop=True,
+            )
+
+        def bank(b):
+            return psum.tile([P, S], F32, name="bank%d" % b)
+
+        e_swin = scale_window("e_swin", 2048, nc.vector)
+        x_swin = scale_window("x_swin", 1024, nc.vector)
+        d_swin = sb("d_swin", [P, 1024], U8)
+        w1_raw, w2_raw, w3_raw, w4_raw = [], [], [], []
+        lab_t = load_list("lab_t", lab)
+        load_scales_spread(d_swin, d_scales, 1024)
+        ovl_t = load_list("ovl_t", ovl)
+        d_win = load_words("d_win", d_words, 1024)
+        w3_raw.append(load_weight_half("w3", w3, 0))
+        load_scales(e_swin, e_scales, nc.sync)
+        w3_raw.append(load_weight_half("w3", w3, 1))
+        w2_raw.append(load_weight_half("w2", w2, 0))
+        w2_raw.append(load_weight_half("w2", w2, 1))
+        offs_t = load_list("offs_t", offs)
+        load_scales(x_swin, x_scales, nc.sync)
+        e_win = load_words("e_win", e_words, 2048)
+        sh1_t = load_list("sh1_t", sh1)
+        unit_t = sb("unit_t", [P, PACK], F32)
+        nc.sync.dma_start(unit_t[:], unit.rearrange("(p t) o -> p (t o)", t=PACK))
+        w1_raw.append(load_weight_half("w1", w1, 0))
+        w1_raw.append(load_weight_half("w1", w1, 1))
+        x_win = load_words("x_win", x_words, 1024)
+        px_t = load_list("px_t", px)
+        w4_raw.append(load_weight_half("w4", w4, 0))
+        w4_raw.append(load_weight_half("w4", w4, 1))
+
+        grouped = {}
+        for name in ("w1", "w2", "w3", "w4"):
+            grouped[name] = sb(name + "_bf16", [P, PACK * K], BF16)
+
+        d_s = gather("d_s", d_swin, lab_t, U8)
+        e_s = gather("e_s", e_swin, ovl_t, U8)
+        x_s = gather("x_s", x_swin, offs_t, U8)
+
+        round_weight_half("scalar", grouped["w3"], w3_raw[0], 0)
+        round_weight_half("scalar", grouped["w3"], w3_raw[1], 1)
+        w3q = quantize("w3", grouped["w3"][:], K)
+        d_c = gather("d_c", d_win, lab_t, U32)
+        yd = [bank(t) for t in range(PACK)]
+        for t in range(PACK):
+            product(yd[t][:], w3q, t, d_c[:], d_s[:])
+
+        round_weight_half("scalar", grouped["w2"], w2_raw[0], 0)
+        round_weight_half("scalar", grouped["w2"], w2_raw[1], 1)
+        w2q = quantize("w2", grouped["w2"][:], K)
+        e_c = gather("e_c", e_win, ovl_t, U32)
+        ye = [bank(PACK + t) for t in range(PACK)]
+        for t in range(PACK):
+            product(ye[t][:], w2q, t, e_c[:], e_s[:])
+
+        alp = sb("alp", [P, PACK, S], F32)
+        for t in range(PACK):
+            nc.scalar.activation(alp[:, t, :], yd[t][:], ACT.Sigmoid, scale=2.0)
+
+        shifted = []
+        for t in range(PACK):
+            over = sb("over%d" % t, [P, S], F32)
+            nc.scalar.activation(over[:], ye[t][:], ACT.Copy, scale=0.8)
+            g = sb("shifted%d" % t, [P, S], F32)
+            for h in range(2):
+                fetch(["scalar","scalar","scalar","scalar"][t], g[:, h * HALF : (h + 1) * HALF], over, sh1_t[:, h * HALF // 16 : (h + 1) * HALF // 16])
+            shifted.append(g)
+
+        neg_unit = sb("neg_unit", [P, PACK], F32)
+        nc.vector.tensor_scalar(neg_unit[:], unit_t[:], -1.0, None, ALU.mult)
+
+        round_weight_half("vector", grouped["w1"], w1_raw[0], 0)
+        round_weight_half("vector", grouped["w1"], w1_raw[1], 1)
+        w1q = quantize("w1", grouped["w1"][:], K)
+        x_c = gather("x_c", x_win, offs_t, U32)
+        y = [bank(PACK + t) for t in range(PACK)]
+        for t in range(PACK):
+            product(y[t][:], w1q, t, x_c[:], x_s[:])
+
+        label = []
+        for t in range(PACK):
+            a = sb("label%d" % t, [P, S], F32)
+            nc.vector.scalar_tensor_tensor(a[:], yd[t][:], unit_t[:, t : t + 1], alp[:, t, :], ALU.mult, ALU.mult)
+            label.append(a)
+
+        picked = [sb("picked%d" % h, [P, PACK, HALF], F32) for h in range(2)]
+        for t in range(PACK):
+            top = sb("top%d" % t, [P, S], F32)
+            nc.vector.tensor_tensor(top[:], y[t][:], shifted[t][:], ALU.max)
+            under = sb("under%d" % t, [P, S], F32)
+            nc.vector.scalar_tensor_tensor(under[:], alp[:, t, :], 1.0, top[:], ALU.subtract, ALU.mult)
+            cov = sb("cov%d" % t, [P, S], F32)
+            nc.vector.scalar_tensor_tensor(cov[:], under[:], neg_unit[:, t : t + 1], label[t][:], ALU.mult, ALU.add)
+            width = [256,256,256,128][t]
+            for c0 in range(0, S, width):
+                fetch(["scalar","scalar","scalar","vector"][t], picked[c0 // HALF][:, t, c0 % HALF : c0 % HALF + width], cov, px_t[:, c0 // 16 : (c0 + width) // 16])
+            if t < 2:
+                round_weight_half(["scalar", "vector"][t], grouped["w4"], w4_raw[t], t)
+        w4q = quantize("w4", grouped["w4"][:], K)
+
+        out_codes = sb("out_codes", [P, S], U32)
+        out_scales = sb("out_scales", [P, S], U8)
+        out_rows = out_0.rearrange("(p t) n -> p t n", t=PACK)
+        out_words = out_1[0].rearrange("p n t -> p (n t)").bitcast(I32)
+        hq = []
+        for c in range(CHUNKS):
+            cols = slice(c * CH, (c + 1) * CH)
+            hid = sb("hid%d" % c, [P, PACK * CH], BF16)
+            nc.vector.tensor_tensor(
+                hid[:].rearrange("p (g i t) -> p g t i", i=4, t=PACK),
+                picked[c * CH // HALF][:, :, c * CH % HALF : c * CH % HALF + CH].rearrange("p t (g i) -> p g t i", i=4),
+                alp[:, :, cols].rearrange("p t (g i) -> p g t i", i=4),
+                ALU.mult,
+            )
+            hq.append(quantize("hid%d" % c, hid[:], CH))
+        for c in range(CHUNKS):
+            cols = slice(c * CH, (c + 1) * CH)
+            res = sb("res%d" % c, [P, PACK, CH], F32)
+            per_bank = S // CH
+            for b in range(PACK // per_bank):
+                acc = bank(c * (PACK // per_bank) + b)
+                for u in range(per_bank):
+                    product(acc[:, u * CH : (u + 1) * CH], w4q, b * per_bank + u, hq[c][0][:], hq[c][1][:])
+                nc.scalar.copy(res[:, b * per_bank : (b + 1) * per_bank, :].rearrange("p t n -> p (t n)"), acc[:])
+            nc.sync.dma_start(out_rows[:, :, cols], res[:])
+            rounded = sb("rounded%d" % c, [P, PACK * CH], BF16)
+            nc.vector.tensor_copy(
+                rounded[:].rearrange("p (g i t) -> p g t i", i=4, t=PACK),
+                res[:].rearrange("p t (g i) -> p g t i", i=4),
+            )
+            nc.vector.quantize_mx(out=out_codes[:, cols].bitcast(FP8X4), scales=out_scales[:, cols], in_=rounded[:])
+            if c % (CHUNKS // 2) == CHUNKS // 2 - 1:
+                half = slice((c + 1) * CH - HALF, (c + 1) * CH)
+                nc.sync.dma_start(out_words[:, half], out_codes[:, half].bitcast(I32))
+        for q in range(4):
+            [nc.sync, nc.scalar][q % 2].dma_start(out_2[0, 4 * q : 4 * q + 4, :].bitcast(I32), out_scales[32 * q : 32 * q + 4, :].bitcast(I32))

@@ -59,15 +59,15 @@ def tile_picked_ymapovl_alpha_po_kernel(
             nc.sync.dma_start(t[:].bitcast(I32), src[0].rearrange("p n t -> p (n t)").bitcast(I32))
             return t
 
-        def load_weight_half(name, w, h):
-            t = sb(name + "_raw%d" % h, [P, PACK, HALF], F32)
-            nc.sync.dma_start(t[:], w.rearrange("(p j) c -> p j c", j=PACK)[:, :, h * HALF : (h + 1) * HALF])
+        def load_weight(name, w):
+            t = sb(name + "_raw", [P, PACK, K], F32)
+            nc.sync.dma_start(t[:], w.rearrange("(p j) c -> p j c", j=PACK))
             return t
 
         def round_weight_half(engine, grouped, raw, h):
             m = HALF // PACK
             dst = grouped[:].rearrange("p (t m j) -> p m t j", t=PACK, j=PACK)[:, h * m : (h + 1) * m]
-            src = raw[:].rearrange("p j (m t) -> p m t j", t=PACK)
+            src = raw[:].rearrange("p j (m t) -> p m t j", t=PACK)[:, h * m : (h + 1) * m]
             if engine == "scalar":
                 nc.scalar.copy(dst, src)
             elif engine == "gpsimd":
@@ -105,28 +105,23 @@ def tile_picked_ymapovl_alpha_po_kernel(
         e_swin = scale_window("e_swin", 2048, nc.vector)
         x_swin = scale_window("x_swin", 1024, nc.vector)
         d_swin = sb("d_swin", [P, 1024], U8)
-        w1_raw, w2_raw, w3_raw, w4_raw = [], [], [], []
         lab_t = load_list("lab_t", lab)
         load_scales_spread(d_swin, d_scales, 1024)
         ovl_t = load_list("ovl_t", ovl)
         d_win = load_words("d_win", d_words, 1024)
-        w3_raw.append(load_weight_half("w3", w3, 0))
+        w3_raw = load_weight("w3", w3)
         load_scales(e_swin, e_scales, nc.sync)
-        w3_raw.append(load_weight_half("w3", w3, 1))
-        w2_raw.append(load_weight_half("w2", w2, 0))
-        w2_raw.append(load_weight_half("w2", w2, 1))
+        w2_raw = load_weight("w2", w2)
         offs_t = load_list("offs_t", offs)
-        load_scales(x_swin, x_scales, nc.sync)
         e_win = load_words("e_win", e_words, 2048)
+        load_scales(x_swin, x_scales, nc.sync)
+        w1_raw = load_weight("w1", w1)
         sh1_t = load_list("sh1_t", sh1)
+        x_win = load_words("x_win", x_words, 1024)
         unit_t = sb("unit_t", [P, PACK], F32)
         nc.sync.dma_start(unit_t[:], unit.rearrange("(p t) o -> p (t o)", t=PACK))
-        w1_raw.append(load_weight_half("w1", w1, 0))
-        w1_raw.append(load_weight_half("w1", w1, 1))
-        x_win = load_words("x_win", x_words, 1024)
         px_t = load_list("px_t", px)
-        w4_raw.append(load_weight_half("w4", w4, 0))
-        w4_raw.append(load_weight_half("w4", w4, 1))
+        w4_raw = load_weight("w4", w4)
 
         grouped = {}
         for name in ("w1", "w2", "w3", "w4"):
@@ -136,16 +131,16 @@ def tile_picked_ymapovl_alpha_po_kernel(
         e_s = gather("e_s", e_swin, ovl_t, U8)
         x_s = gather("x_s", x_swin, offs_t, U8)
 
-        round_weight_half("scalar", grouped["w3"], w3_raw[0], 0)
-        round_weight_half("scalar", grouped["w3"], w3_raw[1], 1)
+        round_weight_half("scalar", grouped["w3"], w3_raw, 0)
+        round_weight_half("vector", grouped["w3"], w3_raw, 1)
         w3q = quantize("w3", grouped["w3"][:], K)
         d_c = gather("d_c", d_win, lab_t, U32)
         yd = [bank(t) for t in range(PACK)]
         for t in range(PACK):
             product(yd[t][:], w3q, t, d_c[:], d_s[:])
 
-        round_weight_half("scalar", grouped["w2"], w2_raw[0], 0)
-        round_weight_half("scalar", grouped["w2"], w2_raw[1], 1)
+        round_weight_half("scalar", grouped["w2"], w2_raw, 0)
+        round_weight_half("vector", grouped["w2"], w2_raw, 1)
         w2q = quantize("w2", grouped["w2"][:], K)
         e_c = gather("e_c", e_win, ovl_t, U32)
         ye = [bank(PACK + t) for t in range(PACK)]
@@ -168,8 +163,8 @@ def tile_picked_ymapovl_alpha_po_kernel(
         neg_unit = sb("neg_unit", [P, PACK], F32)
         nc.vector.tensor_scalar(neg_unit[:], unit_t[:], -1.0, None, ALU.mult)
 
-        round_weight_half("vector", grouped["w1"], w1_raw[0], 0)
-        round_weight_half("vector", grouped["w1"], w1_raw[1], 1)
+        round_weight_half("vector", grouped["w1"], w1_raw, 0)
+        round_weight_half("vector", grouped["w1"], w1_raw, 1)
         w1q = quantize("w1", grouped["w1"][:], K)
         x_c = gather("x_c", x_win, offs_t, U32)
         y = [bank(PACK + t) for t in range(PACK)]
@@ -194,7 +189,7 @@ def tile_picked_ymapovl_alpha_po_kernel(
             for c0 in range(0, S, width):
                 fetch(["scalar","scalar","scalar","vector"][t], picked[c0 // HALF][:, t, c0 % HALF : c0 % HALF + width], cov, px_t[:, c0 // 16 : (c0 + width) // 16])
             if t < 2:
-                round_weight_half(["scalar", "vector"][t], grouped["w4"], w4_raw[t], t)
+                round_weight_half(["scalar", "scalar"][t], grouped["w4"], w4_raw, t)
         w4q = quantize("w4", grouped["w4"][:], K)
 
         out_codes = sb("out_codes", [P, S], U32)
@@ -206,9 +201,9 @@ def tile_picked_ymapovl_alpha_po_kernel(
             cols = slice(c * CH, (c + 1) * CH)
             hid = sb("hid%d" % c, [P, PACK * CH], BF16)
             nc.vector.tensor_tensor(
-                hid[:].rearrange("p (g i t) -> p g t i", i=4, t=PACK),
-                picked[c * CH // HALF][:, :, c * CH % HALF : c * CH % HALF + CH].rearrange("p t (g i) -> p g t i", i=4),
-                alp[:, :, cols].rearrange("p t (g i) -> p g t i", i=4),
+                hid[:].rearrange("p (g i t) -> p g t i", i=2, t=PACK),
+                picked[c * CH // HALF][:, :, c * CH % HALF : c * CH % HALF + CH].rearrange("p t (g i) -> p g t i", i=2),
+                alp[:, :, cols].rearrange("p t (g i) -> p g t i", i=2),
                 ALU.mult,
             )
             hq.append(quantize("hid%d" % c, hid[:], CH))
@@ -224,8 +219,8 @@ def tile_picked_ymapovl_alpha_po_kernel(
             nc.sync.dma_start(out_rows[:, :, cols], res[:])
             rounded = sb("rounded%d" % c, [P, PACK * CH], BF16)
             nc.vector.tensor_copy(
-                rounded[:].rearrange("p (g i t) -> p g t i", i=4, t=PACK),
-                res[:].rearrange("p t (g i) -> p g t i", i=4),
+                rounded[:].rearrange("p (g i t) -> p g t i", i=2, t=PACK),
+                res[:].rearrange("p t (g i) -> p g t i", i=2),
             )
             nc.vector.quantize_mx(out=out_codes[:, cols].bitcast(FP8X4), scales=out_scales[:, cols], in_=rounded[:])
             if c % (CHUNKS // 2) == CHUNKS // 2 - 1:

@@ -165,8 +165,8 @@ def tile_picked_ymapovl_alpha_po_kernel(
 
         round_weight_half("vector", grouped["w1"], w1_raw, 0)
         round_weight_half("vector", grouped["w1"], w1_raw, 1)
-        w1q = quantize("w1", grouped["w1"][:], K)
         x_c = gather("x_c", x_win, offs_t, U32)
+        w1q = quantize("w1", grouped["w1"][:], K)
         y = [bank(PACK + t) for t in range(PACK)]
         for t in range(PACK):
             product(y[t][:], w1q, t, x_c[:], x_s[:])
@@ -177,54 +177,103 @@ def tile_picked_ymapovl_alpha_po_kernel(
             nc.vector.scalar_tensor_tensor(a[:], yd[t][:], unit_t[:, t : t + 1], alp[:, t, :], ALU.mult, ALU.mult)
             label.append(a)
 
+        for h in range(2):
+            round_weight_half("gpsimd", grouped["w4"], w4_raw, h)
+
         picked = [sb("picked%d" % h, [P, PACK, HALF], F32) for h in range(2)]
-        for t in range(PACK):
-            top = sb("top%d" % t, [P, S], F32)
-            nc.vector.tensor_tensor(top[:], y[t][:], shifted[t][:], ALU.max)
-            under = sb("under%d" % t, [P, S], F32)
-            nc.vector.scalar_tensor_tensor(under[:], alp[:, t, :], 1.0, top[:], ALU.subtract, ALU.mult)
+        tops, unders = {}, {}
+
+        def top(t):
+            tops[t] = sb("top%d" % t, [P, S], F32)
+            nc.vector.tensor_tensor(tops[t][:], y[t][:], shifted[t][:], ALU.max)
+
+        def under(t):
+            unders[t] = sb("under%d" % t, [P, S], F32)
+            nc.vector.scalar_tensor_tensor(unders[t][:], alp[:, t, :], 1.0, tops[t][:], ALU.subtract, ALU.mult)
+
+        def cover(t):
             cov = sb("cov%d" % t, [P, S], F32)
-            nc.vector.scalar_tensor_tensor(cov[:], under[:], neg_unit[:, t : t + 1], label[t][:], ALU.mult, ALU.add)
-            width = [256,256,256,128][t]
+            nc.vector.scalar_tensor_tensor(cov[:], unders[t][:], neg_unit[:, t : t + 1], label[t][:], ALU.mult, ALU.add)
+            width = CH if t == PACK - 1 else HALF
             for c0 in range(0, S, width):
-                fetch(["scalar","scalar","scalar","vector"][t], picked[c0 // HALF][:, t, c0 % HALF : c0 % HALF + width], cov, px_t[:, c0 // 16 : (c0 + width) // 16])
-            if t < 2:
-                round_weight_half(["scalar", "scalar"][t], grouped["w4"], w4_raw, t)
+                fetch("scalar", picked[c0 // HALF][:, t, c0 % HALF : c0 % HALF + width], cov, px_t[:, c0 // 16 : (c0 + width) // 16])
+
+        top(0)
+        top(1)
+        under(0)
+        under(1)
+        cover(0)
+        top(2)
+        cover(1)
+        under(2)
+        top(3)
+        cover(2)
+        under(3)
         w4q = quantize("w4", grouped["w4"][:], K)
+        cover(3)
 
         out_codes = sb("out_codes", [P, S], U32)
         out_scales = sb("out_scales", [P, S], U8)
         out_rows = out_0.rearrange("(p t) n -> p t n", t=PACK)
         out_words = out_1[0].rearrange("p n t -> p (n t)").bitcast(I32)
-        hq = []
-        for c in range(CHUNKS):
-            cols = slice(c * CH, (c + 1) * CH)
-            hid = sb("hid%d" % c, [P, PACK * CH], BF16)
+        hids, rounded = {}, {}
+
+        def hidden(c):
+            hids[c] = sb("hid%d" % c, [P, PACK * CH], BF16)
             nc.vector.tensor_tensor(
-                hid[:].rearrange("p (g i t) -> p g t i", i=2, t=PACK),
+                hids[c][:].rearrange("p (g i t) -> p g t i", i=2, t=PACK),
                 picked[c * CH // HALF][:, :, c * CH % HALF : c * CH % HALF + CH].rearrange("p t (g i) -> p g t i", i=2),
-                alp[:, :, cols].rearrange("p t (g i) -> p g t i", i=2),
+                alp[:, :, c * CH : (c + 1) * CH].rearrange("p t (g i) -> p g t i", i=2),
                 ALU.mult,
             )
-            hq.append(quantize("hid%d" % c, hid[:], CH))
-        for c in range(CHUNKS):
+
+        accs, results = {}, {}
+        first_half = sb("res01", [P, PACK, HALF], F32)
+
+        def channels(c):
+            hq = quantize("hid%d" % c, hids[c][:], CH)
+            accs[c] = bank(c)
+            for t in range(PACK):
+                product(accs[c][:, t * CH : (t + 1) * CH], w4q, t, hq[0][:], hq[1][:])
+            if c < 2:
+                results[c] = first_half[:, :, c * CH : (c + 1) * CH]
+            else:
+                results[c] = sb("res%d" % c, [P, PACK, CH], F32)[:]
+            nc.scalar.copy(results[c], accs[c][:].rearrange("p (t n) -> p t n", t=PACK))
+            if c == 1:
+                nc.sync.dma_start(out_rows[:, :, 0:HALF], first_half[:])
+            if c > 1:
+                nc.sync.dma_start(out_rows[:, :, c * CH : (c + 1) * CH], results[c])
+
+        def round_out(c, engine):
+            rounded[c] = sb("rounded%d" % c, [P, PACK * CH], BF16)
+            dst = rounded[c][:].rearrange("p (g i t) -> p g t i", i=2, t=PACK)
+            src = results[c].rearrange("p t (g i) -> p g t i", i=2)
+            if engine == "scalar":
+                nc.scalar.copy(dst, src)
+            else:
+                nc.vector.tensor_copy(dst, src)
+
+        def planes(c):
             cols = slice(c * CH, (c + 1) * CH)
-            res = sb("res%d" % c, [P, PACK, CH], F32)
-            per_bank = S // CH
-            for b in range(PACK // per_bank):
-                acc = bank(c * (PACK // per_bank) + b)
-                for u in range(per_bank):
-                    product(acc[:, u * CH : (u + 1) * CH], w4q, b * per_bank + u, hq[c][0][:], hq[c][1][:])
-                nc.scalar.copy(res[:, b * per_bank : (b + 1) * per_bank, :].rearrange("p t n -> p (t n)"), acc[:])
-            nc.sync.dma_start(out_rows[:, :, cols], res[:])
-            rounded = sb("rounded%d" % c, [P, PACK * CH], BF16)
-            nc.vector.tensor_copy(
-                rounded[:].rearrange("p (g i t) -> p g t i", i=2, t=PACK),
-                res[:].rearrange("p t (g i) -> p g t i", i=2),
-            )
-            nc.vector.quantize_mx(out=out_codes[:, cols].bitcast(FP8X4), scales=out_scales[:, cols], in_=rounded[:])
-            if c % (CHUNKS // 2) == CHUNKS // 2 - 1:
-                half = slice((c + 1) * CH - HALF, (c + 1) * CH)
-                nc.sync.dma_start(out_words[:, half], out_codes[:, half].bitcast(I32))
+            nc.vector.quantize_mx(out=out_codes[:, cols].bitcast(FP8X4), scales=out_scales[:, cols], in_=rounded[c][:])
+
+        hidden(0)
+        hidden(1)
+        channels(0)
+        hidden(2)
+        channels(1)
+        hidden(3)
+        channels(2)
+        round_out(0, "vector")
+        channels(3)
+        round_out(1, "vector")
+        planes(0)
+        round_out(2, "vector")
+        planes(1)
+        round_out(3, "vector")
+        planes(2)
+        planes(3)
+        nc.sync.dma_start(out_words, out_codes[:].bitcast(I32))
         for q in range(4):
             [nc.sync, nc.scalar][q % 2].dma_start(out_2[0, 4 * q : 4 * q + 4, :].bitcast(I32), out_scales[32 * q : 32 * q + 4, :].bitcast(I32))

@@ -124,7 +124,7 @@ def tile_picked_ymapovl_alpha_po_kernel(
         w4_raw = load_weight("w4", w4)
 
         grouped = {}
-        for name in ("w1", "w2", "w3", "w4"):
+        for name in ("w1", "w2", "w3"):
             grouped[name] = sb(name + "_bf16", [P, PACK * K], BF16)
 
         d_s = gather("d_s", d_swin, lab_t, U8)
@@ -177,6 +177,7 @@ def tile_picked_ymapovl_alpha_po_kernel(
             nc.vector.scalar_tensor_tensor(a[:], yd[t][:], unit_t[:, t : t + 1], alp[:, t, :], ALU.mult, ALU.mult)
             label.append(a)
 
+        grouped["w4"] = sb("w1_bf16", [P, PACK * K], BF16)
         for h in range(2):
             round_weight_half("gpsimd", grouped["w4"], w4_raw, h)
 

@@ -14,11 +14,15 @@ ACT = mybir.ActivationFunctionType
 
 P = 128
 PACK = 4
+QUADRANTS = 4
 K = 512
 S = 512
+LIST_ROWS = 16
 HALF = 256
-CHUNKS = 4
-CH = S // CHUNKS
+CHUNK = 128
+CHUNKS = S // CHUNK
+PAIR = 2
+VECTOR_PX_TILE = 2
 
 FLOPS = 4 * 2 * K * K * S
 
@@ -32,249 +36,227 @@ def tile_picked_ymapovl_alpha_po_kernel(
         keep = ctx.enter_context(tc.tile_pool(name="keep", bufs=1))
         psum = ctx.enter_context(tc.psum_pool(name="psum", bufs=1))
 
-        def sb(name, shape, dtype):
+        def sbuf(name, shape, dtype):
             return keep.tile(shape, dtype, name=name, align_bytes=64)
-
-        def load_list(name, src):
-            t = keep.tile([P, S // 16], U16, name=name)
-            nc.sync.dma_start(t[:], src)
-            return t
-
-        def scale_window(name, cols, engine):
-            t = sb(name, [P, cols], U8)
-            engine.memset(t[:].bitcast(I32), 0)
-            return t
-
-        def load_scales_spread(t, src, cols):
-            for q in range(4):
-                rows = src[0, 4 * q : 4 * q + 4, :].bitcast(I32)
-                nc.sync.dma_start(t[32 * q : 32 * q + 32, :].bitcast(I32), rows.unsqueeze(0).broadcast_to([8, 4, cols // 4]))
-
-        def load_scales(t, src, queue):
-            for q in range(4):
-                queue.dma_start(t[32 * q : 32 * q + 4, :].bitcast(I32), src[0, 4 * q : 4 * q + 4, :].bitcast(I32))
-
-        def load_words(name, src, cols):
-            t = sb(name, [P, cols], U32)
-            nc.sync.dma_start(t[:].bitcast(I32), src[0].rearrange("p n t -> p (n t)").bitcast(I32))
-            return t
-
-        def load_weight(name, w):
-            t = sb(name + "_raw", [P, PACK, K], F32)
-            nc.sync.dma_start(t[:], w.rearrange("(p j) c -> p j c", j=PACK))
-            return t
-
-        def round_weight_half(engine, grouped, raw, h):
-            m = HALF // PACK
-            dst = grouped[:].rearrange("p (t m j) -> p m t j", t=PACK, j=PACK)[:, h * m : (h + 1) * m]
-            src = raw[:].rearrange("p j (m t) -> p m t j", t=PACK)[:, h * m : (h + 1) * m]
-            if engine == "scalar":
-                nc.scalar.copy(dst, src)
-            elif engine == "gpsimd":
-                nc.gpsimd.tensor_scalar(dst, src, 1.0, 0.0, ALU.mult, ALU.add)
-            else:
-                nc.vector.tensor_copy(dst, src)
-
-        def fetch(engine, dst, window, offsets):
-            if engine == "scalar":
-                nc.scalar.activation(dst, window[:].indirect(offsets), ACT.Copy)
-            else:
-                nc.vector.tensor_copy(dst, window[:].indirect(offsets))
-
-        def quantize(name, grouped, cols):
-            codes = sb(name + "_codes", [P, cols], U32)
-            scales = sb(name + "_scales", [P, cols], U8)
-            nc.vector.quantize_mx(out=codes[:].bitcast(FP8X4), scales=scales[:], in_=grouped)
-            return codes, scales
-
-        def gather(name, window, offsets, dtype):
-            t = sb(name, [P, S], dtype)
-            nc.vector.tensor_copy(t[:], window[:].indirect(offsets[:]))
-            return t
-
-        def product(dst, w, t, rhs_codes, rhs_scales):
-            cols = slice(t * P, (t + 1) * P)
-            nc.tensor.matmul_mx(
-                out=dst, lhsT=w[0][:, cols].bitcast(FP8X4), lhsT_scale=w[1][:, cols],
-                rhs=rhs_codes.bitcast(FP8X4), rhs_scale=rhs_scales, start=True, stop=True,
-            )
 
         def bank(b):
             return psum.tile([P, S], F32, name="bank%d" % b)
 
-        e_swin = scale_window("e_swin", 2048, nc.vector)
-        x_swin = scale_window("x_swin", 1024, nc.vector)
-        d_swin = sb("d_swin", [P, 1024], U8)
-        lab_t = load_list("lab_t", lab)
-        load_scales_spread(d_swin, d_scales, 1024)
-        ovl_t = load_list("ovl_t", ovl)
-        d_win = load_words("d_win", d_words, 1024)
-        w3_raw = load_weight("w3", w3)
-        load_scales(e_swin, e_scales, nc.sync)
-        w2_raw = load_weight("w2", w2)
-        offs_t = load_list("offs_t", offs)
-        e_win = load_words("e_win", e_words, 2048)
-        load_scales(x_swin, x_scales, nc.sync)
-        w1_raw = load_weight("w1", w1)
-        sh1_t = load_list("sh1_t", sh1)
-        x_win = load_words("x_win", x_words, 1024)
-        unit_t = sb("unit_t", [P, PACK], F32)
-        nc.sync.dma_start(unit_t[:], unit.rearrange("(p t) o -> p (t o)", t=PACK))
-        px_t = load_list("px_t", px)
-        w4_raw = load_weight("w4", w4)
+        def load_list(name, src):
+            offsets = keep.tile([P, S // LIST_ROWS], U16, name=name)
+            nc.sync.dma_start(offsets[:], src)
+            return offsets
 
-        grouped = {}
-        for name in ("w1", "w2", "w3"):
-            grouped[name] = sb(name + "_bf16", [P, PACK * K], BF16)
+        def list_slice(offsets, first, count):
+            return offsets[:, first // LIST_ROWS : (first + count) // LIST_ROWS]
 
-        d_s = gather("d_s", d_swin, lab_t, U8)
-        e_s = gather("e_s", e_swin, ovl_t, U8)
-        x_s = gather("x_s", x_swin, offs_t, U8)
+        def zeroed_scale_table(name, src):
+            table = sbuf(name, [P, src.shape[2]], U8)
+            nc.vector.memset(table[:].bitcast(I32), 0)
+            return table
 
-        round_weight_half("scalar", grouped["w3"], w3_raw, 0)
-        round_weight_half("vector", grouped["w3"], w3_raw, 1)
-        w3q = quantize("w3", grouped["w3"][:], K)
-        d_c = gather("d_c", d_win, lab_t, U32)
+        def load_scale_rows(table, src):
+            for q in range(QUADRANTS):
+                nc.sync.dma_start(table[32 * q : 32 * q + 4, :].bitcast(I32), src[0, 4 * q : 4 * q + 4, :].bitcast(I32))
+
+        def load_scale_rows_repeated(name, src):
+            table = sbuf(name, [P, src.shape[2]], U8)
+            for q in range(QUADRANTS):
+                rows = src[0, 4 * q : 4 * q + 4, :].bitcast(I32)
+                repeated = rows.unsqueeze(0).broadcast_to([8, 4, src.shape[2] // 4])
+                nc.sync.dma_start(table[32 * q : 32 * q + 32, :].bitcast(I32), repeated)
+            return table
+
+        def load_word_table(name, src):
+            table = sbuf(name, [P, src.shape[2]], U32)
+            nc.sync.dma_start(table[:].bitcast(I32), src[0].rearrange("p n t -> p (n t)").bitcast(I32))
+            return table
+
+        def load_weight(name, w):
+            raw = sbuf(name, [P, PACK, K], F32)
+            nc.sync.dma_start(raw[:], w.rearrange("(p j) c -> p j c", j=PACK))
+            return raw
+
+        def weight_half(dealt, raw, h):
+            places = slice(h * HALF // PACK, (h + 1) * HALF // PACK)
+            dst = dealt[:].rearrange("p (t m j) -> p m t j", t=PACK, j=PACK)[:, places]
+            src = raw[:].rearrange("p j (m t) -> p m t j", t=PACK)[:, places]
+            return dst, src
+
+        def quantize(name, values, cols):
+            codes = sbuf(name + "_codes", [P, cols], U32)
+            scales = sbuf(name + "_scales", [P, cols], U8)
+            nc.vector.quantize_mx(out=codes[:].bitcast(FP8X4), scales=scales[:], in_=values[:])
+            return codes, scales
+
+        def pick(name, table, offsets, dtype):
+            picked = sbuf(name, [P, S], dtype)
+            nc.vector.tensor_copy(picked[:], table[:].indirect(offsets[:]))
+            return picked
+
+        def product(dst, weight, t, codes, scales):
+            cols = slice(t * P, (t + 1) * P)
+            nc.tensor.matmul_mx(
+                out=dst, lhsT=weight[0][:, cols].bitcast(FP8X4), lhsT_scale=weight[1][:, cols],
+                rhs=codes[:].bitcast(FP8X4), rhs_scale=scales[:], start=True, stop=True,
+            )
+
+        def interleaved(tile):
+            return tile[:].rearrange("p (g i t) -> p g t i", i=PAIR, t=PACK)
+
+        def by_pairs(tiles):
+            return tiles.rearrange("p t (g i) -> p g t i", i=PAIR)
+
+        e_scale_table = zeroed_scale_table("e_scale_table", e_scales)
+        x_scale_table = zeroed_scale_table("x_scale_table", x_scales)
+        lab_list = load_list("lab_list", lab)
+        d_scale_table = load_scale_rows_repeated("d_scale_table", d_scales)
+        ovl_list = load_list("ovl_list", ovl)
+        d_word_table = load_word_table("d_word_table", d_words)
+        w3_raw = load_weight("w3_raw", w3)
+        load_scale_rows(e_scale_table, e_scales)
+        w2_raw = load_weight("w2_raw", w2)
+        offs_list = load_list("offs_list", offs)
+        e_word_table = load_word_table("e_word_table", e_words)
+        load_scale_rows(x_scale_table, x_scales)
+        w1_raw = load_weight("w1_raw", w1)
+        sh1_list = load_list("sh1_list", sh1)
+        x_word_table = load_word_table("x_word_table", x_words)
+        units = sbuf("units", [P, PACK], F32)
+        nc.sync.dma_start(units[:], unit.rearrange("(p t) o -> p (t o)", t=PACK))
+        px_list = load_list("px_list", px)
+        w4_raw = load_weight("w4_raw", w4)
+
+        warm_in = sbuf("warm_in", [P, 8], F32)
+        nc.gpsimd.memset(warm_in[:], 0.0)
+        warm_out = sbuf("warm_out", [P, 8], F32)
+        nc.scalar.activation(warm_out[:], warm_in[:], ACT.Sigmoid)
+
+        w1_dealt = sbuf("w1_dealt", [P, PACK * K], BF16)
+        w2_dealt = sbuf("w2_dealt", [P, PACK * K], BF16)
+        w3_dealt = sbuf("w3_dealt", [P, PACK * K], BF16)
+
+        d_picked_scales = pick("d_picked_scales", d_scale_table, lab_list, U8)
+        e_picked_scales = pick("e_picked_scales", e_scale_table, ovl_list, U8)
+        x_picked_scales = pick("x_picked_scales", x_scale_table, offs_list, U8)
+
+        nc.scalar.copy(*weight_half(w3_dealt, w3_raw, 0))
+        nc.vector.tensor_copy(*weight_half(w3_dealt, w3_raw, 1))
+        w3_mx = quantize("w3", w3_dealt, K)
+        d_picked_words = pick("d_picked_words", d_word_table, lab_list, U32)
         yd = [bank(t) for t in range(PACK)]
         for t in range(PACK):
-            product(yd[t][:], w3q, t, d_c[:], d_s[:])
+            product(yd[t][:], w3_mx, t, d_picked_words, d_picked_scales)
 
-        round_weight_half("scalar", grouped["w2"], w2_raw, 0)
-        round_weight_half("vector", grouped["w2"], w2_raw, 1)
-        w2q = quantize("w2", grouped["w2"][:], K)
-        e_c = gather("e_c", e_win, ovl_t, U32)
+        nc.scalar.copy(*weight_half(w2_dealt, w2_raw, 0))
+        nc.vector.tensor_copy(*weight_half(w2_dealt, w2_raw, 1))
+        w2_mx = quantize("w2", w2_dealt, K)
+        e_picked_words = pick("e_picked_words", e_word_table, ovl_list, U32)
         ye = [bank(PACK + t) for t in range(PACK)]
         for t in range(PACK):
-            product(ye[t][:], w2q, t, e_c[:], e_s[:])
+            product(ye[t][:], w2_mx, t, e_picked_words, e_picked_scales)
 
-        alp = sb("alp", [P, PACK, S], F32)
+        alp = sbuf("w2_raw", [P, PACK, S], F32)
         for t in range(PACK):
             nc.scalar.activation(alp[:, t, :], yd[t][:], ACT.Sigmoid, scale=2.0)
 
         shifted = []
         for t in range(PACK):
-            over = sb("over%d" % t, [P, S], F32)
-            nc.scalar.activation(over[:], ye[t][:], ACT.Copy, scale=0.8)
-            g = sb("shifted%d" % t, [P, S], F32)
-            for h in range(2):
-                fetch(["scalar","scalar","scalar","scalar"][t], g[:, h * HALF : (h + 1) * HALF], over, sh1_t[:, h * HALF // 16 : (h + 1) * HALF // 16])
-            shifted.append(g)
+            overlay = sbuf("overlay%d" % t, [P, S], F32)
+            nc.scalar.activation(overlay[:], ye[t][:], ACT.Copy, scale=0.8)
+            shifted.append(sbuf("shifted%d" % t, [P, S], F32))
+            for first in range(0, S, HALF):
+                window = overlay[:].indirect(list_slice(sh1_list, first, HALF))
+                nc.scalar.activation(shifted[t][:, first : first + HALF], window, ACT.Copy)
 
-        neg_unit = sb("neg_unit", [P, PACK], F32)
-        nc.vector.tensor_scalar(neg_unit[:], unit_t[:], -1.0, None, ALU.mult)
+        minus_units = sbuf("minus_units", [P, PACK], F32)
+        nc.vector.tensor_scalar(minus_units[:], units[:], -1.0, None, ALU.mult)
 
-        round_weight_half("vector", grouped["w1"], w1_raw, 0)
-        round_weight_half("vector", grouped["w1"], w1_raw, 1)
-        x_c = gather("x_c", x_win, offs_t, U32)
-        w1q = quantize("w1", grouped["w1"][:], K)
+        for h in range(2):
+            nc.vector.tensor_copy(*weight_half(w1_dealt, w1_raw, h))
+        x_picked_words = pick("x_picked_words", x_word_table, offs_list, U32)
+        w1_mx = quantize("w1", w1_dealt, K)
         y = [bank(PACK + t) for t in range(PACK)]
         for t in range(PACK):
-            product(y[t][:], w1q, t, x_c[:], x_s[:])
+            product(y[t][:], w1_mx, t, x_picked_words, x_picked_scales)
 
         label = []
         for t in range(PACK):
-            a = sb("label%d" % t, [P, S], F32)
-            nc.vector.scalar_tensor_tensor(a[:], yd[t][:], unit_t[:, t : t + 1], alp[:, t, :], ALU.mult, ALU.mult)
-            label.append(a)
+            label.append(sbuf("label%d" % t, [P, S], F32))
+            nc.vector.scalar_tensor_tensor(label[t][:], yd[t][:], units[:, t : t + 1], alp[:, t, :], ALU.mult, ALU.mult)
 
-        grouped["w4"] = sb("w1_bf16", [P, PACK * K], BF16)
+        w4_dealt = sbuf("w1_dealt", [P, PACK * K], BF16)
         for h in range(2):
-            round_weight_half("gpsimd", grouped["w4"], w4_raw, h)
+            nc.gpsimd.tensor_scalar(*weight_half(w4_dealt, w4_raw, h), 1.0, 0.0, ALU.mult, ALU.add)
 
-        picked = [sb("picked%d" % h, [P, PACK, HALF], F32) for h in range(2)]
-        tops, unders = {}, {}
+        placed = [sbuf("placed%d" % h, [P, PACK, HALF], F32) for h in range(2)]
+        top, under = {}, {}
 
-        def top(t):
-            tops[t] = sb("top%d" % t, [P, S], F32)
-            nc.vector.tensor_tensor(tops[t][:], y[t][:], shifted[t][:], ALU.max)
+        def larger_layer(t):
+            top[t] = sbuf("top%d" % t, [P, S], F32)
+            nc.vector.tensor_tensor(top[t][:], y[t][:], shifted[t][:], ALU.max)
 
-        def under(t):
-            unders[t] = sb("under%d" % t, [P, S], F32)
-            nc.vector.scalar_tensor_tensor(unders[t][:], alp[:, t, :], 1.0, tops[t][:], ALU.subtract, ALU.mult)
+        def show_through(t):
+            under[t] = sbuf("under%d" % t, [P, S], F32)
+            nc.vector.scalar_tensor_tensor(under[t][:], alp[:, t, :], 1.0, top[t][:], ALU.subtract, ALU.mult)
 
-        def cover(t):
-            cov = sb("cov%d" % t, [P, S], F32)
-            nc.vector.scalar_tensor_tensor(cov[:], unders[t][:], neg_unit[:, t : t + 1], label[t][:], ALU.mult, ALU.add)
-            width = CH if t == PACK - 1 else HALF
-            for c0 in range(0, S, width):
-                fetch("scalar", picked[c0 // HALF][:, t, c0 % HALF : c0 % HALF + width], cov, px_t[:, c0 // 16 : (c0 + width) // 16])
+        def cover_and_place(t):
+            cov = sbuf("cov%d" % t, [P, S], F32)
+            nc.vector.scalar_tensor_tensor(cov[:], under[t][:], minus_units[:, t : t + 1], label[t][:], ALU.mult, ALU.add)
+            count = CHUNK if t == PACK - 1 else HALF
+            for first in range(0, S, count):
+                dst = placed[first // HALF][:, t, first % HALF : first % HALF + count]
+                window = cov[:].indirect(list_slice(px_list, first, count))
+                if t == VECTOR_PX_TILE:
+                    nc.vector.tensor_copy(dst, window)
+                else:
+                    nc.scalar.activation(dst, window, ACT.Copy)
 
-        top(0)
-        top(1)
-        under(0)
-        under(1)
-        cover(0)
-        top(2)
-        cover(1)
-        under(2)
-        top(3)
-        cover(2)
-        under(3)
-        w4q = quantize("w4", grouped["w4"][:], K)
-        cover(3)
+        for pair in ((0, 1), (2, 3)):
+            for step in (larger_layer, show_through, cover_and_place):
+                for t in pair:
+                    step(t)
+        w4_mx = quantize("w4", w4_dealt, K)
 
-        out_codes = sb("out_codes", [P, S], U32)
-        out_scales = sb("out_scales", [P, S], U8)
+        out_codes = sbuf("out_codes", [P, S], U32)
+        out_scales = sbuf("out_scales", [P, S], U8)
         out_rows = out_0.rearrange("(p t) n -> p t n", t=PACK)
-        out_words = out_1[0].rearrange("p n t -> p (n t)").bitcast(I32)
-        hids, rounded = {}, {}
+        hid, result, rounded = {}, {}, {}
 
         def hidden(c):
-            hids[c] = sb("hid%d" % c, [P, PACK * CH], BF16)
+            first = c * CHUNK
+            hid[c] = sbuf("hid%d" % c, [P, PACK * CHUNK], BF16)
             nc.vector.tensor_tensor(
-                hids[c][:].rearrange("p (g i t) -> p g t i", i=2, t=PACK),
-                picked[c * CH // HALF][:, :, c * CH % HALF : c * CH % HALF + CH].rearrange("p t (g i) -> p g t i", i=2),
-                alp[:, :, c * CH : (c + 1) * CH].rearrange("p t (g i) -> p g t i", i=2),
+                interleaved(hid[c]),
+                by_pairs(placed[first // HALF][:, :, first % HALF : first % HALF + CHUNK]),
+                by_pairs(alp[:, :, first : first + CHUNK]),
                 ALU.mult,
             )
 
-        accs, results = {}, {}
-        first_half = sb("res01", [P, PACK, HALF], F32)
-
         def channels(c):
-            hq = quantize("hid%d" % c, hids[c][:], CH)
-            accs[c] = bank(c)
+            hid_codes, hid_scales = quantize("hid%d" % c, hid[c], CHUNK)
+            acc = bank(c)
             for t in range(PACK):
-                product(accs[c][:, t * CH : (t + 1) * CH], w4q, t, hq[0][:], hq[1][:])
-            if c < 2:
-                results[c] = first_half[:, :, c * CH : (c + 1) * CH]
-            else:
-                results[c] = sb("res%d" % c, [P, PACK, CH], F32)[:]
-            nc.scalar.copy(results[c], accs[c][:].rearrange("p (t n) -> p t n", t=PACK))
-            if c == 1:
-                nc.sync.dma_start(out_rows[:, :, 0:HALF], first_half[:])
-            if c > 1:
-                nc.sync.dma_start(out_rows[:, :, c * CH : (c + 1) * CH], results[c])
+                product(acc[:, t * CHUNK : (t + 1) * CHUNK], w4_mx, t, hid_codes, hid_scales)
+            result[c] = sbuf("result%d" % c, [P, PACK, CHUNK], F32)
+            nc.scalar.copy(result[c][:], acc[:].rearrange("p (t n) -> p t n", t=PACK))
+            nc.sync.dma_start(out_rows[:, :, c * CHUNK : (c + 1) * CHUNK], result[c][:])
 
-        def round_out(c, engine):
-            rounded[c] = sb("rounded%d" % c, [P, PACK * CH], BF16)
-            dst = rounded[c][:].rearrange("p (g i t) -> p g t i", i=2, t=PACK)
-            src = results[c].rearrange("p t (g i) -> p g t i", i=2)
-            if engine == "scalar":
-                nc.scalar.copy(dst, src)
-            else:
-                nc.vector.tensor_copy(dst, src)
+        def round_result(c):
+            rounded[c] = sbuf("rounded%d" % c, [P, PACK * CHUNK], BF16)
+            nc.vector.tensor_copy(interleaved(rounded[c]), by_pairs(result[c][:]))
 
-        def planes(c):
-            cols = slice(c * CH, (c + 1) * CH)
+        def quantize_result(c):
+            cols = slice(c * CHUNK, (c + 1) * CHUNK)
             nc.vector.quantize_mx(out=out_codes[:, cols].bitcast(FP8X4), scales=out_scales[:, cols], in_=rounded[c][:])
 
-        hidden(0)
-        hidden(1)
-        channels(0)
-        hidden(2)
-        channels(1)
-        hidden(3)
-        channels(2)
-        round_out(0, "vector")
-        channels(3)
-        round_out(1, "vector")
-        planes(0)
-        round_out(2, "vector")
-        planes(1)
-        round_out(3, "vector")
-        planes(2)
-        planes(3)
-        nc.sync.dma_start(out_words, out_codes[:].bitcast(I32))
-        for q in range(4):
-            [nc.sync, nc.scalar][q % 2].dma_start(out_2[0, 4 * q : 4 * q + 4, :].bitcast(I32), out_scales[32 * q : 32 * q + 4, :].bitcast(I32))
+        stages = ((hidden, 0), (channels, 1), (round_result, 3), (quantize_result, 4))
+        for turn in range(CHUNKS + stages[-1][1]):
+            for stage, behind in stages:
+                if 0 <= turn - behind < CHUNKS:
+                    stage(turn - behind)
+
+        nc.sync.dma_start(out_1[0].rearrange("p n t -> p (n t)").bitcast(I32), out_codes[:].bitcast(I32))
+        for q in range(QUADRANTS):
+            queue = nc.scalar if q % 2 else nc.sync
+            queue.dma_start(out_2[0, 4 * q : 4 * q + 4, :].bitcast(I32), out_scales[32 * q : 32 * q + 4, :].bitcast(I32))

from contextlib import ExitStack

import concourse.mybir as mybir

F32 = mybir.dt.float32
BF16 = mybir.dt.bfloat16
I32 = mybir.dt.int32
U32 = mybir.dt.uint32
U16 = mybir.dt.uint16
U8 = mybir.dt.uint8
FP8X4 = mybir.dt.float8_e4m3fn_x4
ALU = mybir.AluOpType
ACT = mybir.ActivationFunctionType

P = 128
PACK = 4
QUADRANTS = 4
K = 512
S = 512
LIST_ROWS = 16
HALF = 256
CHUNK = 128
CHUNKS = S // CHUNK
PAIR = 2
VECTOR_PX_TILE = 2

FLOPS = 4 * 2 * K * K * S


def tile_picked_ymapovl_alpha_po_kernel(
    tc, x_words, x_scales, w1, e_words, e_scales, w2, d_words, d_scales, w3, unit, w4,
    offs, ovl, lab, sh1, px, out_0, out_1, out_2,
):
    nc = tc.nc
    with ExitStack() as ctx:
        keep = ctx.enter_context(tc.tile_pool(name="keep", bufs=1))
        psum = ctx.enter_context(tc.psum_pool(name="psum", bufs=1))

        def sbuf(name, shape, dtype):
            return keep.tile(shape, dtype, name=name, align_bytes=64)

        def bank(b):
            return psum.tile([P, S], F32, name="bank%d" % b)

        def load_list(name, src):
            offsets = keep.tile([P, S // LIST_ROWS], U16, name=name)
            nc.sync.dma_start(offsets[:], src)
            return offsets

        def list_slice(offsets, first, count):
            return offsets[:, first // LIST_ROWS : (first + count) // LIST_ROWS]

        def zeroed_scale_table(name, src):
            table = sbuf(name, [P, src.shape[2]], U8)
            nc.vector.memset(table[:].bitcast(I32), 0)
            return table

        def load_scale_rows(table, src):
            for q in range(QUADRANTS):
                nc.sync.dma_start(table[32 * q : 32 * q + 4, :].bitcast(I32), src[0, 4 * q : 4 * q + 4, :].bitcast(I32))

        def load_scale_rows_repeated(name, src):
            table = sbuf(name, [P, src.shape[2]], U8)
            for q in range(QUADRANTS):
                rows = src[0, 4 * q : 4 * q + 4, :].bitcast(I32)
                repeated = rows.unsqueeze(0).broadcast_to([8, 4, src.shape[2] // 4])
                nc.sync.dma_start(table[32 * q : 32 * q + 32, :].bitcast(I32), repeated)
            return table

        def load_word_table(name, src):
            table = sbuf(name, [P, src.shape[2]], U32)
            nc.sync.dma_start(table[:].bitcast(I32), src[0].rearrange("p n t -> p (n t)").bitcast(I32))
            return table

        def load_weight(name, w):
            raw = sbuf(name, [P, PACK, K], F32)
            nc.sync.dma_start(raw[:], w.rearrange("(p j) c -> p j c", j=PACK))
            return raw

        def weight_half(dealt, raw, h):
            places = slice(h * HALF // PACK, (h + 1) * HALF // PACK)
            dst = dealt[:].rearrange("p (t m j) -> p m t j", t=PACK, j=PACK)[:, places]
            src = raw[:].rearrange("p j (m t) -> p m t j", t=PACK)[:, places]
            return dst, src

        def quantize(name, values, cols):
            codes = sbuf(name + "_codes", [P, cols], U32)
            scales = sbuf(name + "_scales", [P, cols], U8)
            nc.vector.quantize_mx(out=codes[:].bitcast(FP8X4), scales=scales[:], in_=values[:])
            return codes, scales

        def pick(name, table, offsets, dtype):
            picked = sbuf(name, [P, S], dtype)
            nc.vector.tensor_copy(picked[:], table[:].indirect(offsets[:]))
            return picked

        def product(dst, weight, t, codes, scales):
            cols = slice(t * P, (t + 1) * P)
            nc.tensor.matmul_mx(
                out=dst, lhsT=weight[0][:, cols].bitcast(FP8X4), lhsT_scale=weight[1][:, cols],
                rhs=codes[:].bitcast(FP8X4), rhs_scale=scales[:], start=True, stop=True,
            )

        def interleaved(tile):
            return tile[:].rearrange("p (g i t) -> p g t i", i=PAIR, t=PACK)

        def by_pairs(tiles):
            return tiles.rearrange("p t (g i) -> p g t i", i=PAIR)

        e_scale_table = zeroed_scale_table("e_scale_table", e_scales)
        x_scale_table = zeroed_scale_table("x_scale_table", x_scales)
        lab_list = load_list("lab_list", lab)
        d_scale_table = load_scale_rows_repeated("d_scale_table", d_scales)
        ovl_list = load_list("ovl_list", ovl)
        d_word_table = load_word_table("d_word_table", d_words)
        w3_raw = load_weight("w3_raw", w3)
        load_scale_rows(e_scale_table, e_scales)
        w2_raw = load_weight("w2_raw", w2)
        offs_list = load_list("offs_list", offs)
        e_word_table = load_word_table("e_word_table", e_words)
        load_scale_rows(x_scale_table, x_scales)
        w1_raw = load_weight("w1_raw", w1)
        sh1_list = load_list("sh1_list", sh1)
        x_word_table = load_word_table("x_word_table", x_words)
        units = sbuf("units", [P, PACK], F32)
        nc.sync.dma_start(units[:], unit.rearrange("(p t) o -> p (t o)", t=PACK))
        px_list = load_list("px_list", px)
        w4_raw = load_weight("w4_raw", w4)

        warm_in = sbuf("warm_in", [P, 8], F32)
        nc.gpsimd.memset(warm_in[:], 0.0)
        warm_out = sbuf("warm_out", [P, 8], F32)
        nc.scalar.activation(warm_out[:], warm_in[:], ACT.Sigmoid)

        w1_dealt = sbuf("w1_dealt", [P, PACK * K], BF16)
        w2_dealt = sbuf("w2_dealt", [P, PACK * K], BF16)
        w3_dealt = sbuf("w3_dealt", [P, PACK * K], BF16)

        d_picked_scales = pick("d_picked_scales", d_scale_table, lab_list, U8)
        e_picked_scales = pick("e_picked_scales", e_scale_table, ovl_list, U8)
        x_picked_scales = pick("x_picked_scales", x_scale_table, offs_list, U8)

        nc.scalar.copy(*weight_half(w3_dealt, w3_raw, 0))
        nc.vector.tensor_copy(*weight_half(w3_dealt, w3_raw, 1))
        w3_mx = quantize("w3", w3_dealt, K)
        d_picked_words = pick("d_picked_words", d_word_table, lab_list, U32)
        yd = [bank(t) for t in range(PACK)]
        for t in range(PACK):
            product(yd[t][:], w3_mx, t, d_picked_words, d_picked_scales)

        nc.scalar.copy(*weight_half(w2_dealt, w2_raw, 0))
        nc.vector.tensor_copy(*weight_half(w2_dealt, w2_raw, 1))
        w2_mx = quantize("w2", w2_dealt, K)
        e_picked_words = pick("e_picked_words", e_word_table, ovl_list, U32)
        ye = [bank(PACK + t) for t in range(PACK)]
        for t in range(PACK):
            product(ye[t][:], w2_mx, t, e_picked_words, e_picked_scales)

        alp = sbuf("w2_raw", [P, PACK, S], F32)
        for t in range(PACK):
            nc.scalar.activation(alp[:, t, :], yd[t][:], ACT.Sigmoid, scale=2.0)

        shifted = []
        for t in range(PACK):
            overlay = sbuf("overlay%d" % t, [P, S], F32)
            nc.scalar.activation(overlay[:], ye[t][:], ACT.Copy, scale=0.8)
            shifted.append(sbuf("shifted%d" % t, [P, S], F32))
            for first in range(0, S, HALF):
                window = overlay[:].indirect(list_slice(sh1_list, first, HALF))
                nc.scalar.activation(shifted[t][:, first : first + HALF], window, ACT.Copy)

        minus_units = sbuf("minus_units", [P, PACK], F32)
        nc.vector.tensor_scalar(minus_units[:], units[:], -1.0, None, ALU.mult)

        for h in range(2):
            nc.vector.tensor_copy(*weight_half(w1_dealt, w1_raw, h))
        x_picked_words = pick("x_picked_words", x_word_table, offs_list, U32)
        w1_mx = quantize("w1", w1_dealt, K)
        y = [bank(PACK + t) for t in range(PACK)]
        for t in range(PACK):
            product(y[t][:], w1_mx, t, x_picked_words, x_picked_scales)

        label = []
        for t in range(PACK):
            label.append(sbuf("label%d" % t, [P, S], F32))
            nc.vector.scalar_tensor_tensor(label[t][:], yd[t][:], units[:, t : t + 1], alp[:, t, :], ALU.mult, ALU.mult)

        w4_dealt = sbuf("w1_dealt", [P, PACK * K], BF16)
        for h in range(2):
            nc.gpsimd.tensor_scalar(*weight_half(w4_dealt, w4_raw, h), 1.0, 0.0, ALU.mult, ALU.add)

        placed = [sbuf("placed%d" % h, [P, PACK, HALF], F32) for h in range(2)]
        top, under = {}, {}

        def larger_layer(t):
            top[t] = sbuf("top%d" % t, [P, S], F32)
            nc.vector.tensor_tensor(top[t][:], y[t][:], shifted[t][:], ALU.max)

        def show_through(t):
            under[t] = sbuf("under%d" % t, [P, S], F32)
            nc.vector.scalar_tensor_tensor(under[t][:], alp[:, t, :], 1.0, top[t][:], ALU.subtract, ALU.mult)

        def cover_and_place(t):
            cov = sbuf("cov%d" % t, [P, S], F32)
            nc.vector.scalar_tensor_tensor(cov[:], under[t][:], minus_units[:, t : t + 1], label[t][:], ALU.mult, ALU.add)
            count = CHUNK if t == PACK - 1 else HALF
            for first in range(0, S, count):
                dst = placed[first // HALF][:, t, first % HALF : first % HALF + count]
                window = cov[:].indirect(list_slice(px_list, first, count))
                if t == VECTOR_PX_TILE:
                    nc.vector.tensor_copy(dst, window)
                else:
                    nc.scalar.activation(dst, window, ACT.Copy)

        for pair in ((0, 1), (2, 3)):
            for step in (larger_layer, show_through, cover_and_place):
                for t in pair:
                    step(t)
        w4_mx = quantize("w4", w4_dealt, K)

        out_codes = sbuf("out_codes", [P, S], U32)
        out_scales = sbuf("out_scales", [P, S], U8)
        out_rows = out_0.rearrange("(p t) n -> p t n", t=PACK)
        hid, result, rounded = {}, {}, {}

        def hidden(c):
            first = c * CHUNK
            hid[c] = sbuf("hid%d" % c, [P, PACK * CHUNK], BF16)
            nc.vector.tensor_tensor(
                interleaved(hid[c]),
                by_pairs(placed[first // HALF][:, :, first % HALF : first % HALF + CHUNK]),
                by_pairs(alp[:, :, first : first + CHUNK]),
                ALU.mult,
            )

        def channels(c):
            hid_codes, hid_scales = quantize("hid%d" % c, hid[c], CHUNK)
            acc = bank(c)
            for t in range(PACK):
                product(acc[:, t * CHUNK : (t + 1) * CHUNK], w4_mx, t, hid_codes, hid_scales)
            result[c] = sbuf("result%d" % c, [P, PACK, CHUNK], F32)
            nc.scalar.copy(result[c][:], acc[:].rearrange("p (t n) -> p t n", t=PACK))
            nc.sync.dma_start(out_rows[:, :, c * CHUNK : (c + 1) * CHUNK], result[c][:])

        def round_result(c):
            rounded[c] = sbuf("rounded%d" % c, [P, PACK * CHUNK], BF16)
            nc.vector.tensor_copy(interleaved(rounded[c]), by_pairs(result[c][:]))

        def quantize_result(c):
            cols = slice(c * CHUNK, (c + 1) * CHUNK)
            nc.vector.quantize_mx(out=out_codes[:, cols].bitcast(FP8X4), scales=out_scales[:, cols], in_=rounded[c][:])

        stages = ((hidden, 0), (channels, 1), (round_result, 3), (quantize_result, 4))
        for turn in range(CHUNKS + stages[-1][1]):
            for stage, behind in stages:
                if 0 <= turn - behind < CHUNKS:
                    stage(turn - behind)

        nc.sync.dma_start(out_1[0].rearrange("p n t -> p (n t)").bitcast(I32), out_codes[:].bitcast(I32))
        for q in range(QUADRANTS):
            queue = nc.scalar if q % 2 else nc.sync
            queue.dma_start(out_2[0, 4 * q : 4 * q + 4, :].bitcast(I32), out_scales[32 * q : 32 * q + 4, :].bitcast(I32))
